import numpy as np
import ml_dtypes


def mxq(x, axis, fmt="e4m3"):
    dtype, down = {"e4m3": (ml_dtypes.float8_e4m3fn, 7), "e5m2": (ml_dtypes.float8_e5m2, 14)}[fmt]
    v = np.moveaxis(np.asarray(x, np.float32).astype(ml_dtypes.bfloat16).astype(np.float64), axis, -1)
    blocks = v.reshape(v.shape[:-1] + (-1, 32))
    amax = np.abs(blocks).max(-1, keepdims=True)
    byte = np.maximum(np.where(amax > 0, np.frexp(amax)[1] - 1 + 127, 0) - down, 1)
    scale = np.exp2(byte - 127.0)
    codes = (blocks / scale).astype(np.float32).astype(dtype).astype(np.float64)
    return np.moveaxis((codes * scale).reshape(v.shape), -1, axis)


WIDE = False


def mx_kscale(k, group=512):
    if not WIDE:
        return np.ones(k)
    levels = np.array([18, -18])
    if group != 512:
        return np.exp2(np.random.permutation(np.resize(levels, k // group))).repeat(group)
    if k % 512:
        return np.exp2(np.random.permutation(np.resize(levels, k // 32))).repeat(32)
    a = np.empty((k // 512, 16))
    for p in range(k // 512):
        a[p, :8] = np.random.permutation(np.resize(levels, 8))
        for g in range(8):
            far = levels[np.abs(levels - a[p, g]) >= 10]
            a[p, g + 8] = far[np.random.randint(len(far))]
    return np.exp2(a.ravel()).repeat(32)


def f64(x):
    return np.asarray(x).astype(np.float64)


def softplus(v):
    return np.log(1.0 + np.exp(v))


def sigmoid(v):
    return 1.0 / (1.0 + np.exp(-v))


G, D, M, N = 4, 128, 128, 512


def setup_inputs():
    n = np.random.standard_normal
    s_d = mx_kscale(D, 0)
    return {
        "x": (n((G, D, N)) * s_d[:, None]).astype(np.float32),
        "w1": (n((G, D, M)) / np.sqrt(D) / s_d[:, None]).astype(np.float32),
        "w2": (n((G, D, M)) / np.sqrt(D) / s_d[:, None]).astype(np.float32),
        "hp1": (np.random.uniform(0.3, 1.0, (G, M, 1))).astype(np.float32),
        "dx": (n((G, D, N)) * s_d[:, None]).astype(np.float32),
        "og": (np.random.uniform(0.5, 2.0, (G, M, 1))).astype(np.float32),
        "base": (0.3 * n((G, M, N))).astype(np.float32),
    }


def reference(x, w1, w2, hp1, dx, og, base):
    w1q = mxq(f64(w1), 1, "e4m3")
    xq = mxq(f64(x), 1, "e4m3")
    z1 = w1q.transpose(0, 2, 1) @ xq
    dxq = mxq(f64(dx), 1, "e4m3")
    tz1 = w1q.transpose(0, 2, 1) @ dxq
    w2q = mxq(f64(w2), 1, "e4m3")
    z2 = w2q.transpose(0, 2, 1) @ xq
    tz2 = w2q.transpose(0, 2, 1) @ dxq
    q1 = np.square(softplus(z1))
    xq1 = tz1 * sigmoid(z1) * softplus(z1) * 2.0
    xh = (xq1 - (xq1 + tz2 * sigmoid(z2)) * q1 / (q1 + softplus(z2) + f64(hp1))) / (q1 + softplus(z2) + f64(hp1)) * 2.0
    y = xh * f64(og) + f64(base)
    return y

@@ -1,0 +1,239 @@
+import math
+from contextlib import ExitStack
+
+import concourse.mybir as mybir
+
+G, D, M, N = 4, 128, 128, 512
+FLOPS = 4 * 2 * G * D * M * N
+
+F32 = mybir.dt.float32
+BF16 = mybir.dt.bfloat16
+U32 = mybir.dt.uint32
+U8 = mybir.dt.uint8
+FP8X4 = mybir.dt.float8_e4m3fn_x4
+ACT = mybir.ActivationFunctionType
+ALU = mybir.AluOpType
+
+P = 128
+PACK = 4
+ROWS = D // PACK
+HALF = N // 2
+MM_N = 128
+RUN = 4
+LN_SHIFT = 43.5
+LN_FLOOR = 2.0 ** -64
+
+
+def tile_rows_tnhill_kernel(tc, x, w1, w2, hp1, dx, og, base, out):
+    nc = tc.nc
+    with ExitStack() as ctx:
+        sb = ctx.enter_context(tc.tile_pool(name="sb", bufs=1))
+        ps = ctx.enter_context(tc.psum_pool(name="ps", bufs=1))
+        ctx.enter_context(tc.manual_schedule())
+
+        def f32(name, *shape):
+            return sb.tile([P, *shape], F32, name=name, align_bytes=64)
+
+        def operand(name, src):
+            width = src.shape[2]
+            return {
+                "src": src,
+                "raw": f32(name + "_raw", PACK, width),
+                "packed": sb.tile([P, width, PACK], BF16, name=name + "_packed", align_bytes=64),
+                "codes": sb.tile([P, width], U32, name=name + "_codes", align_bytes=64),
+                "scales": sb.tile([P, width], U8, name=name + "_scales", align_bytes=64),
+            }
+
+        def by_rows(t):
+            return t.rearrange("g (p j) n -> (g p) j n", j=PACK)
+
+        halves = [slice(h * HALF, (h + 1) * HALF) for h in range(2)]
+        xs = [operand("x%d" % h, by_rows(x)[:, :, halves[h]]) for h in range(2)]
+        dxs = [operand("dx%d" % h, by_rows(dx)[:, :, halves[h]]) for h in range(2)]
+        ws = [operand("w1", by_rows(w1)), operand("w2", by_rows(w2))]
+
+        half_point = f32("half_point", G, 8)
+        gain = f32("gain", G, 8)
+        half_shifted = f32("half_shifted", G)
+        warm = f32("warm", 8)
+        warm_out = f32("warm_out", 8)
+        bank = [[ps.tile([P, 2, HALF], F32, name="bank%d%d" % (g, h)) for h in range(2)] for g in range(G)]
+        names2 = ("nsig", "tsig", "lg")
+        names1 = ("bas", "sq", "den", "lnden", "rec", "p1", "p2", "num", "num2", "y", "res")
+        t = {nm: [f32("%s%d" % (nm, g), 2, N) for g in range(G)] for nm in names2}
+        t.update({nm: [f32("%s%d" % (nm, g), N) for g in range(G)] for nm in names1})
+
+        def load(op):
+            nc.sync.dma_start(out=op["raw"][:], in_=op["src"])
+
+        def pack(op, engine, cols=None):
+            width = op["src"].shape[2]
+            cols = cols or slice(0, width)
+            dst = op["packed"][:, cols, :].rearrange("p (c i) j -> p c j i", i=RUN)
+            src = op["raw"][:, :, cols].rearrange("p j (c i) -> p c j i", i=RUN)
+            if engine == "vector":
+                nc.vector.tensor_copy(out=dst, in_=src)
+            else:
+                nc.scalar.copy(out=dst, in_=src)
+
+        def quantize(op):
+            nc.vector.quantize_mx(
+                out=op["codes"][:].bitcast(FP8X4),
+                scales=op["scales"][:],
+                in_=op["packed"][:].rearrange("p n j -> p (n j)"),
+            )
+
+        def product(g, h, k, moving, c):
+            rows = slice(g * ROWS, (g + 1) * ROWS)
+            cols = slice(c * MM_N, (c + 1) * MM_N)
+            nc.tensor.matmul_mx(
+                out=bank[g][h][:, k, cols],
+                lhsT=ws[k]["codes"][rows, :].bitcast(FP8X4),
+                lhsT_scale=ws[k]["scales"][rows, :],
+                rhs=moving["codes"][rows, cols].bitcast(FP8X4),
+                rhs_scale=moving["scales"][rows, cols],
+                start=True,
+                stop=True,
+            )
+
+        chunks = range(HALF // MM_N)
+
+        def products(g, h, moving):
+            for k in range(2):
+                for c in chunks:
+                    product(g, h, k, moving, c)
+
+        def sigmoid(g, h):
+            nc.scalar.activation(out=t["nsig"][g][:, :, halves[h]], in_=bank[g][h][:], func=ACT.Sigmoid, scale=-1.0)
+
+        def tangent(g, h):
+            nc.vector.scalar_tensor_tensor(
+                out=t["tsig"][g][:, :, halves[h]], in0=t["nsig"][g][:, :, halves[h]], scalar=1.0,
+                in1=bank[g][h][:], op0=ALU.subtract, op1=ALU.mult)
+
+        def stt(dst, in0, scalar, in1, op0, op1):
+            nc.vector.scalar_tensor_tensor(out=dst, in0=in0, scalar=scalar, in1=in1, op0=op0, op1=op1)
+
+        def log_k(g, k):
+            nc.scalar.activation(out=t["lg"][g][:, k, :], in_=t["nsig"][g][:, k, :], func=ACT.Ln,
+                                 scale=math.exp(LN_SHIFT), bias=LN_FLOOR)
+
+        def logs(g):
+            log_k(g, 1)
+            log_k(g, 0)
+            nc.scalar.activation(out=t["sq"][g][:], in_=t["lg"][g][:, 0, :], func=ACT.Square, bias=-LN_SHIFT)
+
+        def log_den(g):
+            nc.scalar.activation(out=t["lnden"][g][:], in_=t["den"][g][:], func=ACT.Ln, scale=math.sqrt(0.5))
+
+        def recip(g):
+            nc.scalar.activation(out=t["rec"][g][:], in_=t["lnden"][g][:], func=ACT.Exp, scale=-2.0)
+
+        def p1(g):
+            stt(t["p1"][g][:], t["lg"][g][:, 1, :], half_shifted[:, g:g + 1], t["tsig"][g][:, 0, :], ALU.subtract, ALU.mult)
+
+        def p2(g):
+            stt(t["p2"][g][:], t["lg"][g][:, 0, :], LN_SHIFT, t["tsig"][g][:, 1, :], ALU.subtract, ALU.mult)
+
+        def den(g):
+            stt(t["den"][g][:], t["sq"][g][:], half_shifted[:, g:g + 1], t["lg"][g][:, 1, :], ALU.add, ALU.subtract)
+
+        def num(g):
+            stt(t["num"][g][:], t["p1"][g][:], 2.0, t["p2"][g][:], ALU.mult, ALU.subtract)
+
+        def num2(g):
+            stt(t["num2"][g][:], t["lg"][g][:, 0, :], LN_SHIFT, t["num"][g][:], ALU.subtract, ALU.mult)
+
+        def y(g):
+            stt(t["y"][g][:], t["num2"][g][:], gain[:, g, 0:1], t["rec"][g][:], ALU.mult, ALU.mult)
+
+        def finish(g):
+            nc.vector.tensor_tensor(out=t["res"][g][:], in0=t["bas"][g][:], in1=t["y"][g][:], op=ALU.subtract)
+            nc.sync.dma_start(out=out[g], in_=t["res"][g][:])
+
+        for op in (xs[0], ws[0], ws[1], xs[1], dxs[0], dxs[1]):
+            load(op)
+        with nc.allow_non_contiguous_dma(reason="one value a partition"):
+            nc.sync.dma_start(out=half_point[:, :, 0:1], in_=hp1.rearrange("g m o -> m g o"))
+            nc.sync.dma_start(out=gain[:, :, 0:1], in_=og.rearrange("g m o -> m g o"))
+        for g in range(G):
+            nc.sync.dma_start(out=t["bas"][g][:], in_=base[g])
+
+        nc.gpsimd.memset(warm[:], 0.0)
+        nc.scalar.activation(out=warm_out[:], in_=warm[:], func=ACT.Sigmoid)
+        nc.gpsimd.tensor_scalar(out=half_shifted[:], in0=half_point[:, :, 0], scalar1=LN_SHIFT, scalar2=1.0,
+                                op0=ALU.add, op1=ALU.mult)
+
+        pack(xs[0], "vector")
+        pack(ws[0], "scalar")
+        quantize(xs[0])
+        pack(ws[1], "vector", slice(0, 64))
+        pack(ws[1], "scalar", slice(64, 128))
+        quantize(ws[0])
+        quantize(ws[1])
+        for c in chunks:
+            for g in range(G):
+                product(g, 0, 0, xs[0], c)
+        for g in range(G):
+            for c in chunks:
+                product(g, 0, 1, xs[0], c)
+        pack(xs[1], "vector")
+        for g in range(G):
+            sigmoid(g, 0)
+        quantize(xs[1])
+        for g in range(G):
+            products(g, 1, xs[1])
+        pack(dxs[0], "vector")
+        for g in range(G):
+            sigmoid(g, 1)
+        quantize(dxs[0])
+        for g in range(G):
+            products(g, 0, dxs[0])
+        pack(dxs[1], "vector")
+        tangent(0, 0)
+        quantize(dxs[1])
+        for g in range(G):
+            products(g, 1, dxs[1])
+        for g in range(1, G):
+            tangent(g, 0)
+        for g in range(G):
+            tangent(g, 1)
+
+        logs(0)
+        p1(0)
+        p2(0)
+        den(0)
+        num(0)
+        logs(1)
+        p1(1)
+        num2(0)
+        log_den(0)
+        den(1)
+        p2(1)
+        logs(2)
+        p1(2)
+        num(1)
+        log_den(1)
+        den(2)
+        num2(1)
+        p2(2)
+        logs(3)
+        den(3)
+        log_den(2)
+        log_den(3)
+        num(2)
+        p1(3)
+        num2(2)
+        p2(3)
+        for g in range(G):
+            recip(g)
+        y(0)
+        num(3)
+        finish(0)
+        num2(3)
+        y(1)
+        y(2)
+        finish(1)
+        y(3)
+        finish(2)
+        finish(3)

@@ -36,12 +36,13 @@ def tile_rows_tnhill_kernel(tc, x, w1, w2, hp1, dx, og, base, out):
 
         def operand(name, src):
             width = src.shape[2]
+            pieces = range(width // MM_N)
             return {
                 "src": src,
                 "raw": f32(name + "_raw", PACK, width),
-                "packed": sb.tile([P, width, PACK], BF16, name=name + "_packed", align_bytes=64),
-                "codes": sb.tile([P, width], U32, name=name + "_codes", align_bytes=64),
-                "scales": sb.tile([P, width], U8, name=name + "_scales", align_bytes=64),
+                "packed": [sb.tile([P, MM_N, PACK], BF16, name="%s_packed%d" % (name, c), align_bytes=64) for c in pieces],
+                "codes": [sb.tile([P, MM_N], U32, name="%s_codes%d" % (name, c), align_bytes=64) for c in pieces],
+                "scales": [sb.tile([P, MM_N], U8, name="%s_scales%d" % (name, c), align_bytes=64) for c in pieces],
             }
 
         def by_rows(t):
@@ -66,42 +67,40 @@ def tile_rows_tnhill_kernel(tc, x, w1, w2, hp1, dx, og, base, out):
         def load(op):
             nc.sync.dma_start(out=op["raw"][:], in_=op["src"])
 
-        def pack(op, engine, cols=None):
-            width = op["src"].shape[2]
-            cols = cols or slice(0, width)
-            dst = op["packed"][:, cols, :].rearrange("p (c i) j -> p c j i", i=RUN)
-            src = op["raw"][:, :, cols].rearrange("p j (c i) -> p c j i", i=RUN)
-            if engine == "vector":
-                nc.vector.tensor_copy(out=dst, in_=src)
-            else:
-                nc.scalar.copy(out=dst, in_=src)
-
-        def quantize(op):
-            nc.vector.quantize_mx(
-                out=op["codes"][:].bitcast(FP8X4),
-                scales=op["scales"][:],
-                in_=op["packed"][:].rearrange("p n j -> p (n j)"),
-            )
-
-        def product(g, h, k, moving, c):
-            rows = slice(g * ROWS, (g + 1) * ROWS)
+        def pack(op, c, copy):
             cols = slice(c * MM_N, (c + 1) * MM_N)
-            nc.tensor.matmul_mx(
-                out=bank[g][h][:, k, cols],
-                lhsT=ws[k]["codes"][rows, :].bitcast(FP8X4),
-                lhsT_scale=ws[k]["scales"][rows, :],
-                rhs=moving["codes"][rows, cols].bitcast(FP8X4),
-                rhs_scale=moving["scales"][rows, cols],
-                start=True,
-                stop=True,
+            copy(out=op["packed"][c][:].rearrange("p (r i) j -> p r j i", i=RUN),
+                 in_=op["raw"][:, :, cols].rearrange("p j (r i) -> p r j i", i=RUN))
+
+        def quantize(op, c):
+            nc.vector.quantize_mx(
+                out=op["codes"][c][:].bitcast(FP8X4),
+                scales=op["scales"][c][:],
+                in_=op["packed"][c][:].rearrange("p n j -> p (n j)"),
             )
 
         chunks = range(HALF // MM_N)
 
-        def products(g, h, moving):
+        def prepare(op):
+            for c in chunks:
+                pack(op, c, nc.vector.tensor_copy)
+            for c in chunks:
+                quantize(op, c)
+
+        def products(h, moving):
             for k in range(2):
                 for c in chunks:
-                    product(g, h, k, moving, c)
+                    for g in range(G):
+                        rows = slice(g * ROWS, (g + 1) * ROWS)
+                        nc.tensor.matmul_mx(
+                            out=bank[g][h][:, k, c * MM_N:(c + 1) * MM_N],
+                            lhsT=ws[k]["codes"][0][rows, :].bitcast(FP8X4),
+                            lhsT_scale=ws[k]["scales"][0][rows, :],
+                            rhs=moving["codes"][c][rows, :].bitcast(FP8X4),
+                            rhs_scale=moving["scales"][c][rows, :],
+                            start=True,
+                            stop=True,
+                        )
 
         def sigmoid(g, h):
             nc.scalar.activation(out=t["nsig"][g][:, :, halves[h]], in_=bank[g][h][:], func=ACT.Sigmoid, scale=-1.0)
@@ -144,12 +143,12 @@ def tile_rows_tnhill_kernel(tc, x, w1, w2, hp1, dx, og, base, out):
         def num2(g):
             stt(t["num2"][g][:], t["lg"][g][:, 0, :], LN_SHIFT, t["num"][g][:], ALU.subtract, ALU.mult)
 
-        def y(g):
-            stt(t["y"][g][:], t["num2"][g][:], gain[:, g, 0:1], t["rec"][g][:], ALU.mult, ALU.mult)
+        def y(g, cols=slice(0, N)):
+            stt(t["y"][g][:, cols], t["num2"][g][:, cols], gain[:, g, 0:1], t["rec"][g][:, cols], ALU.mult, ALU.mult)
 
-        def finish(g):
-            nc.vector.tensor_tensor(out=t["res"][g][:], in0=t["bas"][g][:], in1=t["y"][g][:], op=ALU.subtract)
-            nc.sync.dma_start(out=out[g], in_=t["res"][g][:])
+        def finish(g, cols=slice(0, N)):
+            nc.vector.tensor_tensor(out=t["res"][g][:, cols], in0=t["bas"][g][:, cols], in1=t["y"][g][:, cols], op=ALU.subtract)
+            nc.sync.dma_start(out=out[g][:, cols], in_=t["res"][g][:, cols])
 
         for op in (xs[0], ws[0], ws[1], xs[1], dxs[0], dxs[1]):
             load(op)
@@ -164,40 +163,24 @@ def tile_rows_tnhill_kernel(tc, x, w1, w2, hp1, dx, og, base, out):
         nc.gpsimd.tensor_scalar(out=half_shifted[:], in0=half_point[:, :, 0], scalar1=LN_SHIFT, scalar2=1.0,
                                 op0=ALU.add, op1=ALU.mult)
 
-        pack(xs[0], "vector")
-        pack(ws[0], "scalar")
-        quantize(xs[0])
-        pack(ws[1], "vector", slice(0, 64))
-        pack(ws[1], "scalar", slice(64, 128))
-        quantize(ws[0])
-        quantize(ws[1])
-        for c in chunks:
+        prepare(xs[0])
+        pack(ws[0], 0, nc.scalar.copy)
+        pack(ws[1], 0, nc.vector.tensor_copy)
+        quantize(ws[0], 0)
+        quantize(ws[1], 0)
+        products(0, xs[0])
+        prepare(xs[1])
+        products(1, xs[1])
+        for h in range(2):
             for g in range(G):
-                product(g, 0, 0, xs[0], c)
-        for g in range(G):
-            for c in chunks:
-                product(g, 0, 1, xs[0], c)
-        pack(xs[1], "vector")
-        for g in range(G):
-            sigmoid(g, 0)
-        quantize(xs[1])
-        for g in range(G):
-            products(g, 1, xs[1])
-        pack(dxs[0], "vector")
-        for g in range(G):
-            sigmoid(g, 1)
-        quantize(dxs[0])
-        for g in range(G):
-            products(g, 0, dxs[0])
-        pack(dxs[1], "vector")
-        tangent(0, 0)
-        quantize(dxs[1])
-        for g in range(G):
-            products(g, 1, dxs[1])
-        for g in range(1, G):
-            tangent(g, 0)
-        for g in range(G):
-            tangent(g, 1)
+                sigmoid(g, h)
+        prepare(dxs[0])
+        products(0, dxs[0])
+        prepare(dxs[1])
+        products(1, dxs[1])
+        for h in range(2):
+            for g in range(G):
+                tangent(g, h)
 
         logs(0)
         p1(0)
@@ -236,4 +219,5 @@ def tile_rows_tnhill_kernel(tc, x, w1, w2, hp1, dx, og, base, out):
         finish(1)
         y(3)
         finish(2)
-        finish(3)
+        finish(3, halves[0])
+        finish(3, halves[1])

@@ -53,8 +53,8 @@ def tile_rows_tnhill_kernel(tc, x, w1, w2, hp1, dx, og, base, out):
         dxs = [operand("dx%d" % h, by_rows(dx)[:, :, halves[h]]) for h in range(2)]
         ws = [operand("w1", by_rows(w1)), operand("w2", by_rows(w2))]
 
-        half_point = f32("half_point", G, 8)
-        gain = f32("gain", G, 8)
+        rows_in = f32("rows_in", G * ROWS)
+        columns = f32("columns", G, ROWS)
         half_shifted = f32("half_shifted", G)
         warm = f32("warm", 8)
         warm_out = f32("warm_out", 8)
@@ -87,20 +87,22 @@ def tile_rows_tnhill_kernel(tc, x, w1, w2, hp1, dx, og, base, out):
             for c in chunks:
                 quantize(op, c)
 
-        def products(h, moving):
+        def product(g, h, k, c, moving):
+            rows = slice(g * ROWS, (g + 1) * ROWS)
+            nc.tensor.matmul_mx(
+                out=bank[g][h][:, k, c * MM_N:(c + 1) * MM_N],
+                lhsT=ws[k]["codes"][0][rows, :].bitcast(FP8X4),
+                lhsT_scale=ws[k]["scales"][0][rows, :],
+                rhs=moving["codes"][c][rows, :].bitcast(FP8X4),
+                rhs_scale=moving["scales"][c][rows, :],
+                start=True,
+                stop=True,
+            )
+
+        def products(g, h, moving):
             for k in range(2):
                 for c in chunks:
-                    for g in range(G):
-                        rows = slice(g * ROWS, (g + 1) * ROWS)
-                        nc.tensor.matmul_mx(
-                            out=bank[g][h][:, k, c * MM_N:(c + 1) * MM_N],
-                            lhsT=ws[k]["codes"][0][rows, :].bitcast(FP8X4),
-                            lhsT_scale=ws[k]["scales"][0][rows, :],
-                            rhs=moving["codes"][c][rows, :].bitcast(FP8X4),
-                            rhs_scale=moving["scales"][c][rows, :],
-                            start=True,
-                            stop=True,
-                        )
+                    product(g, h, k, c, moving)
 
         def sigmoid(g, h):
             nc.scalar.activation(out=t["nsig"][g][:, :, halves[h]], in_=bank[g][h][:], func=ACT.Sigmoid, scale=-1.0)
@@ -144,43 +146,57 @@ def tile_rows_tnhill_kernel(tc, x, w1, w2, hp1, dx, og, base, out):
             stt(t["num2"][g][:], t["lg"][g][:, 0, :], LN_SHIFT, t["num"][g][:], ALU.subtract, ALU.mult)
 
         def y(g, cols=slice(0, N)):
-            stt(t["y"][g][:, cols], t["num2"][g][:, cols], gain[:, g, 0:1], t["rec"][g][:, cols], ALU.mult, ALU.mult)
+            stt(t["y"][g][:, cols], t["num2"][g][:, cols], columns[:, g, 1:2], t["rec"][g][:, cols], ALU.mult, ALU.mult)
 
         def finish(g, cols=slice(0, N)):
             nc.vector.tensor_tensor(out=t["res"][g][:, cols], in0=t["bas"][g][:, cols], in1=t["y"][g][:, cols], op=ALU.subtract)
             nc.sync.dma_start(out=out[g][:, cols], in_=t["res"][g][:, cols])
 
-        for op in (xs[0], ws[0], ws[1], xs[1], dxs[0], dxs[1]):
+        nc.gpsimd.memset(warm[:], 0.0)
+        nc.gpsimd.memset(rows_in[:], 0.0)
+
+        for op in (ws[0], xs[0], ws[1], xs[1], dxs[0], dxs[1]):
             load(op)
-        with nc.allow_non_contiguous_dma(reason="one value a partition"):
-            nc.sync.dma_start(out=half_point[:, :, 0:1], in_=hp1.rearrange("g m o -> m g o"))
-            nc.sync.dma_start(out=gain[:, :, 0:1], in_=og.rearrange("g m o -> m g o"))
+        for place, vec in enumerate((hp1, og)):
+            nc.sync.dma_start(out=rows_in[place:P:ROWS, :].rearrange("a (g i) -> a g i", g=G),
+                              in_=vec.rearrange("g (a i) o -> a g (i o)", i=ROWS))
         for g in range(G):
             nc.sync.dma_start(out=t["bas"][g][:], in_=base[g])
 
-        nc.gpsimd.memset(warm[:], 0.0)
         nc.scalar.activation(out=warm_out[:], in_=warm[:], func=ACT.Sigmoid)
-        nc.gpsimd.tensor_scalar(out=half_shifted[:], in0=half_point[:, :, 0], scalar1=LN_SHIFT, scalar2=1.0,
-                                op0=ALU.add, op1=ALU.mult)
 
-        prepare(xs[0])
-        pack(ws[0], 0, nc.scalar.copy)
-        pack(ws[1], 0, nc.vector.tensor_copy)
+        pack(ws[0], 0, nc.vector.tensor_copy)
         quantize(ws[0], 0)
+        pack(xs[0], 0, nc.vector.tensor_copy)
+        pack(xs[0], 1, nc.scalar.copy)
+        quantize(xs[0], 0)
+        pack(ws[1], 0, nc.vector.tensor_copy)
+        quantize(xs[0], 1)
         quantize(ws[1], 0)
-        products(0, xs[0])
+        for c in chunks:
+            for g in range(G):
+                product(g, 0, 0, c, xs[0])
+        for g in range(G):
+            for c in chunks:
+                product(g, 0, 1, c, xs[0])
         prepare(xs[1])
-        products(1, xs[1])
+        for g in range(G):
+            products(g, 1, xs[1])
         for h in range(2):
             for g in range(G):
                 sigmoid(g, h)
         prepare(dxs[0])
-        products(0, dxs[0])
         prepare(dxs[1])
-        products(1, dxs[1])
+        nc.vector.transpose(out=columns[:].rearrange("p g i -> p (g i)"), in_=rows_in[:])
         for h in range(2):
             for g in range(G):
-                tangent(g, h)
+                products(g, h, dxs[h])
+        tangent(0, 0)
+        nc.vector.tensor_scalar(out=half_shifted[:], in0=columns[:, :, 0], scalar1=LN_SHIFT, scalar2=None, op0=ALU.add)
+        for g in range(1, G):
+            tangent(g, 0)
+        for g in range(G):
+            tangent(g, 1)
 
         logs(0)
         p1(0)
@@ -189,35 +205,34 @@ def tile_rows_tnhill_kernel(tc, x, w1, w2, hp1, dx, og, base, out):
         num(0)
         logs(1)
         p1(1)
-        num2(0)
-        log_den(0)
         den(1)
+        num2(0)
         p2(1)
         logs(2)
-        p1(2)
-        num(1)
-        log_den(1)
+        log_den(0)
         den(2)
+        num(1)
+        p1(2)
         num2(1)
-        p2(2)
         logs(3)
         den(3)
+        log_den(1)
         log_den(2)
         log_den(3)
-        num(2)
+        p2(2)
         p1(3)
-        num2(2)
+        num(2)
         p2(3)
+        num2(2)
+        num(3)
         for g in range(G):
             recip(g)
         y(0)
-        num(3)
-        finish(0)
         num2(3)
+        finish(0)
         y(1)
         y(2)
         finish(1)
         y(3)
         finish(2)
-        finish(3, halves[0])
-        finish(3, halves[1])
+        finish(3)

import math
from contextlib import ExitStack

import concourse.mybir as mybir

G, D, M, N = 4, 128, 128, 512
FLOPS = 4 * 2 * G * D * M * N

F32 = mybir.dt.float32
BF16 = mybir.dt.bfloat16
U32 = mybir.dt.uint32
U8 = mybir.dt.uint8
FP8X4 = mybir.dt.float8_e4m3fn_x4
ACT = mybir.ActivationFunctionType
ALU = mybir.AluOpType

P = 128
PACK = 4
ROWS = D // PACK
HALF = N // 2
MM_N = 128
RUN = 4
LN_SHIFT = 43.5
LN_FLOOR = 2.0 ** -64


def tile_rows_tnhill_kernel(tc, x, w1, w2, hp1, dx, og, base, out):
    nc = tc.nc
    with ExitStack() as ctx:
        sb = ctx.enter_context(tc.tile_pool(name="sb", bufs=1))
        ps = ctx.enter_context(tc.psum_pool(name="ps", bufs=1))
        ctx.enter_context(tc.manual_schedule())

        def f32(name, *shape):
            return sb.tile([P, *shape], F32, name=name, align_bytes=64)

        def operand(name, src):
            width = src.shape[2]
            pieces = range(width // MM_N)
            return {
                "src": src,
                "raw": f32(name + "_raw", PACK, width),
                "packed": [sb.tile([P, MM_N, PACK], BF16, name="%s_packed%d" % (name, c), align_bytes=64) for c in pieces],
                "codes": [sb.tile([P, MM_N], U32, name="%s_codes%d" % (name, c), align_bytes=64) for c in pieces],
                "scales": [sb.tile([P, MM_N], U8, name="%s_scales%d" % (name, c), align_bytes=64) for c in pieces],
            }

        def by_rows(t):
            return t.rearrange("g (p j) n -> (g p) j n", j=PACK)

        halves = [slice(h * HALF, (h + 1) * HALF) for h in range(2)]
        xs = [operand("x%d" % h, by_rows(x)[:, :, halves[h]]) for h in range(2)]
        dxs = [operand("dx%d" % h, by_rows(dx)[:, :, halves[h]]) for h in range(2)]
        ws = [operand("w1", by_rows(w1)), operand("w2", by_rows(w2))]

        rows_in = f32("rows_in", G * ROWS)
        columns = f32("columns", G, ROWS)
        half_shifted = f32("half_shifted", G)
        warm = f32("warm", 8)
        warm_out = f32("warm_out", 8)
        bank = [[ps.tile([P, 2, HALF], F32, name="bank%d%d" % (g, h)) for h in range(2)] for g in range(G)]
        names2 = ("nsig", "tsig", "lg")
        names1 = ("bas", "sq", "den", "lnden", "rec", "p1", "p2", "num", "num2", "y", "res")
        t = {nm: [f32("%s%d" % (nm, g), 2, N) for g in range(G)] for nm in names2}
        t.update({nm: [f32("%s%d" % (nm, g), N) for g in range(G)] for nm in names1})

        def load(op):
            nc.sync.dma_start(out=op["raw"][:], in_=op["src"])

        def pack(op, c, copy):
            cols = slice(c * MM_N, (c + 1) * MM_N)
            copy(out=op["packed"][c][:].rearrange("p (r i) j -> p r j i", i=RUN),
                 in_=op["raw"][:, :, cols].rearrange("p j (r i) -> p r j i", i=RUN))

        def quantize(op, c):
            nc.vector.quantize_mx(
                out=op["codes"][c][:].bitcast(FP8X4),
                scales=op["scales"][c][:],
                in_=op["packed"][c][:].rearrange("p n j -> p (n j)"),
            )

        chunks = range(HALF // MM_N)

        def prepare(op):
            for c in chunks:
                pack(op, c, nc.vector.tensor_copy)
            for c in chunks:
                quantize(op, c)

        def product(g, h, k, c, moving):
            rows = slice(g * ROWS, (g + 1) * ROWS)
            nc.tensor.matmul_mx(
                out=bank[g][h][:, k, c * MM_N:(c + 1) * MM_N],
                lhsT=ws[k]["codes"][0][rows, :].bitcast(FP8X4),
                lhsT_scale=ws[k]["scales"][0][rows, :],
                rhs=moving["codes"][c][rows, :].bitcast(FP8X4),
                rhs_scale=moving["scales"][c][rows, :],
                start=True,
                stop=True,
            )

        def products(g, h, moving):
            for k in range(2):
                for c in chunks:
                    product(g, h, k, c, moving)

        def sigmoid(g, h):
            nc.scalar.activation(out=t["nsig"][g][:, :, halves[h]], in_=bank[g][h][:], func=ACT.Sigmoid, scale=-1.0)

        def tangent(g, h):
            nc.vector.scalar_tensor_tensor(
                out=t["tsig"][g][:, :, halves[h]], in0=t["nsig"][g][:, :, halves[h]], scalar=1.0,
                in1=bank[g][h][:], op0=ALU.subtract, op1=ALU.mult)

        def stt(dst, in0, scalar, in1, op0, op1):
            nc.vector.scalar_tensor_tensor(out=dst, in0=in0, scalar=scalar, in1=in1, op0=op0, op1=op1)

        def log_k(g, k):
            nc.scalar.activation(out=t["lg"][g][:, k, :], in_=t["nsig"][g][:, k, :], func=ACT.Ln,
                                 scale=math.exp(LN_SHIFT), bias=LN_FLOOR)

        def logs(g):
            log_k(g, 1)
            log_k(g, 0)
            nc.scalar.activation(out=t["sq"][g][:], in_=t["lg"][g][:, 0, :], func=ACT.Square, bias=-LN_SHIFT)

        def log_den(g):
            nc.scalar.activation(out=t["lnden"][g][:], in_=t["den"][g][:], func=ACT.Ln, scale=math.sqrt(0.5))

        def recip(g):
            nc.scalar.activation(out=t["rec"][g][:], in_=t["lnden"][g][:], func=ACT.Exp, scale=-2.0)

        def p1(g):
            stt(t["p1"][g][:], t["lg"][g][:, 1, :], half_shifted[:, g:g + 1], t["tsig"][g][:, 0, :], ALU.subtract, ALU.mult)

        def p2(g):
            stt(t["p2"][g][:], t["lg"][g][:, 0, :], LN_SHIFT, t["tsig"][g][:, 1, :], ALU.subtract, ALU.mult)

        def den(g):
            stt(t["den"][g][:], t["sq"][g][:], half_shifted[:, g:g + 1], t["lg"][g][:, 1, :], ALU.add, ALU.subtract)

        def num(g):
            stt(t["num"][g][:], t["p1"][g][:], 2.0, t["p2"][g][:], ALU.mult, ALU.subtract)

        def num2(g):
            stt(t["num2"][g][:], t["lg"][g][:, 0, :], LN_SHIFT, t["num"][g][:], ALU.subtract, ALU.mult)

        def y(g, cols=slice(0, N)):
            stt(t["y"][g][:, cols], t["num2"][g][:, cols], columns[:, g, 1:2], t["rec"][g][:, cols], ALU.mult, ALU.mult)

        def finish(g, cols=slice(0, N)):
            nc.vector.tensor_tensor(out=t["res"][g][:, cols], in0=t["bas"][g][:, cols], in1=t["y"][g][:, cols], op=ALU.subtract)
            nc.sync.dma_start(out=out[g][:, cols], in_=t["res"][g][:, cols])

        nc.gpsimd.memset(warm[:], 0.0)
        nc.gpsimd.memset(rows_in[:], 0.0)

        for op in (ws[0], xs[0], ws[1], xs[1], dxs[0], dxs[1]):
            load(op)
        for place, vec in enumerate((hp1, og)):
            nc.sync.dma_start(out=rows_in[place:P:ROWS, :].rearrange("a (g i) -> a g i", g=G),
                              in_=vec.rearrange("g (a i) o -> a g (i o)", i=ROWS))
        for g in range(G):
            nc.sync.dma_start(out=t["bas"][g][:], in_=base[g])

        nc.scalar.activation(out=warm_out[:], in_=warm[:], func=ACT.Sigmoid)

        pack(ws[0], 0, nc.vector.tensor_copy)
        quantize(ws[0], 0)
        pack(xs[0], 0, nc.vector.tensor_copy)
        pack(xs[0], 1, nc.scalar.copy)
        quantize(xs[0], 0)
        pack(ws[1], 0, nc.vector.tensor_copy)
        quantize(xs[0], 1)
        quantize(ws[1], 0)
        for c in chunks:
            for g in range(G):
                product(g, 0, 0, c, xs[0])
        for g in range(G):
            for c in chunks:
                product(g, 0, 1, c, xs[0])
        prepare(xs[1])
        for g in range(G):
            products(g, 1, xs[1])
        for h in range(2):
            for g in range(G):
                sigmoid(g, h)
        prepare(dxs[0])
        prepare(dxs[1])
        nc.vector.transpose(out=columns[:].rearrange("p g i -> p (g i)"), in_=rows_in[:])
        for h in range(2):
            for g in range(G):
                products(g, h, dxs[h])
        tangent(0, 0)
        nc.vector.tensor_scalar(out=half_shifted[:], in0=columns[:, :, 0], scalar1=LN_SHIFT, scalar2=None, op0=ALU.add)
        for g in range(1, G):
            tangent(g, 0)
        for g in range(G):
            tangent(g, 1)

        logs(0)
        p1(0)
        p2(0)
        den(0)
        num(0)
        logs(1)
        p1(1)
        den(1)
        num2(0)
        p2(1)
        logs(2)
        log_den(0)
        den(2)
        num(1)
        p1(2)
        num2(1)
        logs(3)
        den(3)
        log_den(1)
        log_den(2)
        log_den(3)
        p2(2)
        p1(3)
        num(2)
        p2(3)
        num2(2)
        num(3)
        for g in range(G):
            recip(g)
        y(0)
        num2(3)
        finish(0)
        y(1)
        y(2)
        finish(1)
        y(3)
        finish(2)
        finish(3)
